import numpy as np
import ml_dtypes


def mxq(x, axis, fmt="e4m3"):
    dtype, down = {"e4m3": (ml_dtypes.float8_e4m3fn, 7), "e5m2": (ml_dtypes.float8_e5m2, 14)}[fmt]
    v = np.moveaxis(np.asarray(x, np.float32).astype(ml_dtypes.bfloat16).astype(np.float64), axis, -1)
    blocks = v.reshape(v.shape[:-1] + (-1, 32))
    amax = np.abs(blocks).max(-1, keepdims=True)
    byte = np.maximum(np.where(amax > 0, np.frexp(amax)[1] - 1 + 127, 0) - down, 1)
    scale = np.exp2(byte - 127.0)
    codes = (blocks / scale).astype(np.float32).astype(dtype).astype(np.float64)
    return np.moveaxis((codes * scale).reshape(v.shape), -1, axis)


WIDE = False


def mx_kscale(k):
    if not WIDE:
        return np.ones(k)
    levels = np.array([10, -10, 5, -5, 0])
    if k % 512:
        return np.exp2(np.random.permutation(np.resize(levels, k // 32))).repeat(32)
    a = np.empty((k // 512, 16))
    for p in range(k // 512):
        a[p, :8] = np.random.permutation(np.resize(levels, 8))
        for g in range(8):
            far = levels[np.abs(levels - a[p, g]) >= 10]
            a[p, g + 8] = far[np.random.randint(len(far))]
    return np.exp2(a.ravel()).repeat(32)


def f64(x):
    return np.asarray(x).astype(np.float64)


def striped(idx):
    return np.tile(idx.reshape(-1, 16).T, (8, 1)).astype(np.uint16)


def unstriped(offs):
    return offs[:16].T.reshape(-1).astype(np.int64)


E2M1 = np.array([0.0, 0.5, 1.0, 1.5, 2.0, 3.0, 4.0, 6.0, -0.0, -0.5, -1.0, -1.5, -2.0, -3.0, -4.0, -6.0])


def pack_weight(w, fmt):
    k, n = w.shape
    w = f64(np.asarray(w, np.float32).astype(ml_dtypes.bfloat16)).reshape(k // 32, 32, n)
    amax = np.abs(w).max(1)
    if fmt == "e4m3":
        byte = np.frexp(amax)[1] - 1 + 127 - 7
    else:
        mant, ex = np.frexp(amax / 6.0)
        byte = np.where(mant > 0.5, ex, ex - 1) + 127
    byte = np.clip(np.where(amax > 0, byte, 1), 1, 254)
    scaled = (w * np.exp2(127.0 - byte)[:, None, :]).reshape(k, n).astype(np.float32)
    by_word = np.ascontiguousarray(scaled.reshape(k // 512, 128, 4, n).transpose(0, 1, 3, 2))
    if fmt == "e4m3":
        words = by_word.astype(ml_dtypes.float8_e4m3fn).view(np.uint8)
    else:
        c = by_word.astype(ml_dtypes.float4_e2m1fn).view(np.uint8) & 0xF
        words = (c[..., 0::2] | (c[..., 1::2] << 4)).reshape(k // 512, 128, 2 * n)
    return np.ascontiguousarray(words), np.ascontiguousarray(byte.astype(np.uint8).reshape(k // 512, 16, n))


def unpack_weight(words, scales, fmt):
    g, _, n = scales.shape
    words = np.ascontiguousarray(words).reshape(g, 128, n, -1)
    if fmt == "e4m3":
        vals = words.view(ml_dtypes.float8_e4m3fn).astype(np.float64)
    else:
        nib = np.empty((g, 128, n, 4), np.uint8)
        nib[..., 0::2] = words & 0xF
        nib[..., 1::2] = words >> 4
        vals = E2M1[nib]
    vals = vals * np.repeat(np.exp2(scales.astype(np.float64) - 127.0), 8, axis=1)[..., None]
    return vals.transpose(0, 1, 3, 2).reshape(g * 512, n)


def planes(y):
    n, m = y.shape
    v = y.astype(np.float32).astype(ml_dtypes.bfloat16).astype(np.float64).reshape(n // 32, 32, m)
    top = np.abs(v).max(1)
    byte = np.clip(np.where(top > 0, np.frexp(top)[1] - 1 + 127 - 7, 1), 1, 254)
    codes = (v * np.exp2(127.0 - byte)[:, None, :]).reshape(n, m).astype(np.float32).astype(ml_dtypes.float8_e4m3fn).view(np.uint8)
    words = codes.reshape(n // 512, 128, 4, m).transpose(0, 1, 3, 2)
    return np.ascontiguousarray(words), np.ascontiguousarray(byte.astype(np.uint8).reshape(n // 512, 16, m))


def relu2(v):
    return np.maximum(v, 0.0) ** 2


K, T, E, C, H, N, HOT = 1536, 640, 5, 256, 512, 512, 1


def by_expert(wq, xq):
    return np.concatenate([wq[e].T @ xq[:, e * C:(e + 1) * C] for e in range(E)], axis=1)


def setup_inputs():
    n = np.random.standard_normal
    s = mx_kscale(K)
    u = mx_kscale(H)
    slot_token = np.concatenate([np.random.permutation(T)[:C] for e in range(E)])
    x = pack_weight(n((K, T)) * s[:, None], "e4m3")
    w1h = [pack_weight(m, "e4m3") for m in n((HOT, K, H)) / np.sqrt(K) / s[None, :, None] * u]
    w2h = [pack_weight(m, "e4m3") for m in n((HOT, H, N)) / np.sqrt(H) / u[None, :, None] ** 2]
    w1c = [pack_weight(m, "e2m1") for m in n((E - HOT, K, H)) / np.sqrt(K) / s[None, :, None] * u]
    w2c = [pack_weight(m, "e2m1") for m in n((E - HOT, H, N)) / np.sqrt(H) / u[None, :, None] ** 2]
    return {
        "x_words": x[0],
        "x_scales": x[1],
        "w1h_words": np.stack([m[0] for m in w1h]),
        "w1h_scales": np.stack([m[1] for m in w1h]),
        "w2h_words": np.stack([m[0] for m in w2h]),
        "w2h_scales": np.stack([m[1] for m in w2h]),
        "w1c_words": np.stack([m[0] for m in w1c]),
        "w1c_scales": np.stack([m[1] for m in w1c]),
        "w2c_words": np.stack([m[0] for m in w2c]),
        "w2c_scales": np.stack([m[1] for m in w2c]),
        "offs": striped(slot_token),
    }


def reference(x_words, x_scales, w1h_words, w1h_scales, w2h_words, w2h_scales, w1c_words, w1c_scales, w2c_words, w2c_scales, offs):
    w1h = np.stack([unpack_weight(w1h_words[e], w1h_scales[e], "e4m3") for e in range(HOT)])
    w2h = np.stack([unpack_weight(w2h_words[e], w2h_scales[e], "e4m3") for e in range(HOT)])
    w1c = np.stack([unpack_weight(w1c_words[e], w1c_scales[e], "e2m1") for e in range(E - HOT)])
    w2c = np.stack([unpack_weight(w2c_words[e], w2c_scales[e], "e2m1") for e in range(E - HOT)])
    idx = unstriped(offs)
    xq = unpack_weight(x_words, x_scales, "e4m3")[:, idx]
    w1 = [*w1h, *w1c]
    w2 = [*w2h, *w2c]
    h = relu2(by_expert(w1, xq))
    y = by_expert(w2, mxq(h, 0, "e4m3"))
    out = y
    out_0 = out
    return (out_0,) + planes(out_0)

@@ -1,0 +1,222 @@
+from contextlib import ExitStack
+
+import concourse.mybir as mybir
+from concourse.masks import make_identity
+
+K, T, E, C, H, N = 1536, 640, 5, 256, 512, 512
+S = E * C
+FLOPS = 2 * S * (K * H + H * N)
+
+F32 = mybir.dt.float32
+BF16 = mybir.dt.bfloat16
+I32 = mybir.dt.int32
+U32 = mybir.dt.uint32
+U16 = mybir.dt.uint16
+U8 = mybir.dt.uint8
+FP8X4 = mybir.dt.float8_e4m3fn_x4
+FP4X4 = mybir.dt.float4_e2m1fn_x4
+ACT = mybir.ActivationFunctionType
+
+P = 128
+PACK = 4
+PASSES = K // (P * PACK)
+COLD = E - 1
+ORDER = [1, 2, 3, 4, 0]
+REGION = 4096
+BANK = 2048
+W1_BASE = (E + 2) * REGION
+W1_COLD_BYTES = PASSES * H * 2
+
+
+def load_scale_rows(queue, tile, rows):
+    planes = rows.shape[0]
+    for q in range(4):
+        queue.dma_start(
+            out=tile[32 * q : 32 * q + 4, :].bitcast(I32).rearrange("r (a w) -> r a w", a=planes),
+            in_=rows[:, 4 * q : 4 * q + 4, :].bitcast(I32).rearrange("a r w -> r a w"),
+        )
+
+
+def tile_moe_hot_s_mlp_relu2_kernel(
+    tc, x_words, x_scales, w1h_words, w1h_scales, w2h_words, w2h_scales, w1c_words, w1c_scales, w2c_words, w2c_scales, offs,
+    out_0, out_1, out_2,
+):
+    nc = tc.nc
+    with ExitStack() as ctx:
+        lists = ctx.enter_context(tc.tile_pool(name="lists", bufs=1))
+        keep = ctx.enter_context(tc.tile_pool(name="keep", bufs=1))
+        shared = ctx.enter_context(tc.tile_pool(name="shared", bufs=1))
+        ring = ctx.enter_context(tc.tile_pool(name="ring", bufs=6))
+        psum1 = ctx.enter_context(tc.psum_pool(name="psum1", bufs=1))
+        psum2 = ctx.enter_context(tc.psum_pool(name="psum2", bufs=4))
+
+        offsets = lists.tile([P, S // 16], U16, name="offsets")
+        nc.sync.dma_start(offsets[:], offs)
+
+        xs = keep.tile([P, PASSES * T], U8, name="xs", align_bytes=64)
+        nc.vector.memset(xs[:].bitcast(I32), 0)
+        load_scale_rows(nc.scalar, xs, x_scales)
+
+        xw = keep.tile([P, PASSES * T], U32, name="xw", align_bytes=64)
+        nc.sync.dma_start(
+            out=xw[:].bitcast(I32).rearrange("p (s t) -> p s t", s=PASSES),
+            in_=x_words.rearrange("s p t d -> p s (t d)").bitcast(I32),
+        )
+
+        w1 = {}
+
+        def load_w1(pos):
+            e = ORDER[pos]
+            if e == 0:
+                t = shared.tile([P, PASSES * H * 4], U8, name="w1_hot", align_bytes=64, offset=W1_BASE + W1_COLD_BYTES)
+                src = w1h_words[0].rearrange("s p i d -> p s (i d)")
+            else:
+                t = shared.tile([P, W1_COLD_BYTES], U8, name="w1_cold%d" % pos, align_bytes=64,
+                                offset=W1_BASE + W1_COLD_BYTES * ((pos + 1) % 2))
+                src = w1c_words[e - 1].rearrange("s p c -> p s c")
+            nc.sync.dma_start(out=t[:].bitcast(I32).rearrange("p (s w) -> p s w", s=PASSES), in_=src.bitcast(I32))
+            w1[pos] = t
+
+        load_w1(0)
+        w1cs = keep.tile([P, COLD * PASSES * H], U8, name="w1cs", align_bytes=64)
+        nc.vector.memset(w1cs[:].bitcast(I32), 0)
+        load_scale_rows(nc.sync, w1cs, w1c_scales.rearrange("f s b i -> (f s) b i"))
+        load_w1(1)
+
+        w2cs_raw = keep.tile([P, COLD * N], U8, name="w2cs_raw", align_bytes=64)
+        nc.gpsimd.memset(w2cs_raw[:].bitcast(I32), 0)
+        load_scale_rows(nc.sync, w2cs_raw, w2c_scales.rearrange("f s b i -> (f s) b i"))
+        w2hs_raw = keep.tile([P, N], U8, name="w2hs_raw", align_bytes=64)
+        nc.gpsimd.memset(w2hs_raw[:].bitcast(I32), 0)
+        w1hs = keep.tile([P, PASSES * H], U8, name="w1hs", align_bytes=64)
+        nc.gpsimd.memset(w1hs[:].bitcast(I32), 0)
+        load_scale_rows(nc.sync, w1hs, w1h_scales[0])
+        load_scale_rows(nc.sync, w2hs_raw, w2h_scales[0])
+        ident = keep.tile([P, P], F32, name="ident")
+        make_identity(nc, ident[:])
+
+        y_scales = keep.tile([P, S], U8, name="y_scales", align_bytes=64)
+        out_rows = out_0.rearrange("(p t) j -> p t j", t=PACK)
+        out_words = out_1[0].rearrange("p j d -> p (j d)").bitcast(I32)
+
+        gw, gs, hb, hq, ysb, w2raw, w2, w2s = {}, {}, {}, {}, {}, {}, {}, {}
+
+        def pieces(pos):
+            return [(0, P), (P, P)] if pos == E - 1 else [(0, C)]
+
+        def gather(pos):
+            e = ORDER[pos]
+            gs[pos] = shared.tile([P, PASSES * C], U8, name="gs%d" % pos, align_bytes=64, offset=pos * REGION)
+            gw[pos] = shared.tile([P, PASSES * C], U32, name="gw%d" % pos, align_bytes=64, offset=pos * REGION + 1024)
+            idx = offsets[:, e * C // 16 : (e + 1) * C // 16]
+            for s in range(PASSES):
+                nc.vector.tensor_copy(out=gs[pos][:, s * C : (s + 1) * C], in_=xs[:, s * T : (s + 1) * T].indirect(idx))
+            for j0, n in pieces(pos):
+                idx = offsets[:, (e * C + j0) // 16 : (e * C + j0 + n) // 16]
+                for s in range(PASSES):
+                    nc.vector.tensor_copy(out=gw[pos][:, s * C + j0 : s * C + j0 + n],
+                                          in_=xw[:, s * T : (s + 1) * T].indirect(idx))
+
+        def first_layer(pos):
+            e = ORDER[pos]
+            hb[pos] = shared.tile([P, C * PACK], BF16, name="hb%d" % pos, align_bytes=64, offset=(pos + 2) * REGION)
+            for half in range(C // P):
+                acc = psum1.tile([P, H], F32, name="acc1_%d_%d" % (pos, half), offset=BANK * ((pos + half) % 3))
+                for s in range(PASSES):
+                    cols = slice(s * C + half * P, s * C + (half + 1) * P)
+                    if e == 0:
+                        rhs = w1[pos][:, s * H * 4 : (s + 1) * H * 4].bitcast(FP8X4)
+                        rhs_scale = w1hs[:, s * H : (s + 1) * H]
+                    else:
+                        rhs = w1[pos][:, s * H * 2 : (s + 1) * H * 2].bitcast(FP4X4)
+                        a = (e - 1) * PASSES + s
+                        rhs_scale = w1cs[:, a * H : (a + 1) * H]
+                    nc.tensor.matmul_mx(out=acc[:], lhsT=gw[pos][:, cols].bitcast(FP8X4), lhsT_scale=gs[pos][:, cols],
+                                        rhs=rhs, rhs_scale=rhs_scale, start=(s == 0), stop=(s == PASSES - 1))
+                relu = ring.tile([P, PACK, P], F32, name="relu")
+                nc.scalar.activation(out=relu[:], in_=acc[:].rearrange("j (m t) -> j t m", t=PACK), func=ACT.Relu)
+                turned = psum1.tile([P, PACK, P], F32, name="turned_%d_%d" % (pos, half),
+                                    offset=BANK * ((pos + 2) % 3 if half == 0 else 3))
+                for t in range(PACK):
+                    nc.tensor.transpose(turned[:, t, :], relu[:, t, :], ident[:])
+                nc.scalar.activation(
+                    out=hb[pos][:, half * P * PACK : (half + 1) * P * PACK].rearrange("m (j t) -> m j t", t=PACK),
+                    in_=turned[:].rearrange("m t j -> m j t"), func=ACT.Square)
+
+        def quantise_h(pos):
+            for j0, n in pieces(pos):
+                codes = ring.tile([P, n], U32, name="h_codes", align_bytes=64)
+                scales = ring.tile([P, n], U8, name="h_scales", align_bytes=64)
+                nc.vector.quantize_mx(out=codes[:].bitcast(FP8X4), scales=scales[:], in_=hb[pos][:, j0 * PACK : (j0 + n) * PACK])
+                hq[pos, j0] = (codes, scales)
+
+        def deal_w2(pos):
+            e = ORDER[pos]
+            w2s[pos] = keep.tile([P, N], U8, name="w2s%d" % pos, align_bytes=64)
+            raw = w2hs_raw[:] if e == 0 else w2cs_raw[:, (e - 1) * N : e * N]
+            nc.gpsimd.tensor_copy(out=w2s[pos][:].rearrange("p (t m) -> p t m", t=PACK),
+                                  in_=raw.rearrange("p (m t) -> p t m", t=PACK))
+            if e == 0:
+                w2[pos] = keep.tile([P, N], U32, name="w2_%d" % pos, align_bytes=64)
+                nc.scalar.copy(out=w2[pos][:].rearrange("p (t m) -> p t m", t=PACK),
+                               in_=w2raw["hot"][:].rearrange("p (m t) -> p t m", t=PACK))
+            else:
+                w2[pos] = keep.tile([P, N * 2], U8, name="w2_%d" % pos, align_bytes=64)
+                wc = slice((e - 1) * N * 2, e * N * 2)
+                nc.scalar.copy(out=w2[pos][:].bitcast(U16).rearrange("p (t m) -> p t m", t=PACK),
+                               in_=w2raw["cold"][:, wc].bitcast(U16).rearrange("p (m t) -> p t m", t=PACK))
+
+        def second_layer(pos, j0, n):
+            e = ORDER[pos]
+            codes, scales = hq[pos, j0]
+            ysb[pos, j0] = ring.tile([P, PACK, n], F32, name="ysb")
+            per_bank = N // n
+            for t0 in range(0, PACK, per_bank):
+                acc = psum2.tile([P, per_bank, n], F32, name="acc2")
+                for u in range(per_bank):
+                    t = t0 + u
+                    if e == 0:
+                        lhsT = w2[pos][:, t * P : (t + 1) * P].bitcast(FP8X4)
+                    else:
+                        lhsT = w2[pos][:, 2 * t * P : 2 * (t + 1) * P].bitcast(FP4X4)
+                    nc.tensor.matmul_mx(out=acc[:, u, :], lhsT=lhsT, lhsT_scale=w2s[pos][:, t * P : (t + 1) * P],
+                                        rhs=codes[:].bitcast(FP8X4), rhs_scale=scales[:], start=True, stop=True)
+                nc.scalar.copy(out=ysb[pos, j0][:, t0 : t0 + per_bank, :], in_=acc[:])
+            nc.sync.dma_start(out=out_rows[:, :, e * C + j0 : e * C + j0 + n], in_=ysb[pos, j0][:])
+
+        def planes(pos, j0, n, slot):
+            e = ORDER[pos]
+            cols = slice(e * C + j0, e * C + j0 + n)
+            yb = shared.tile([P, n * PACK], BF16, name="yb%d_%d" % (pos, j0), align_bytes=64,
+                             offset=(E - 1) * REGION + 2048 * slot)
+            nc.vector.tensor_copy(out=yb[:].rearrange("p (c i t) -> p c t i", i=4, t=PACK),
+                                  in_=ysb[pos, j0][:].rearrange("p t (c i) -> p c t i", i=4))
+            y_codes = ring.tile([P, n], U32, name="y_codes", align_bytes=64)
+            nc.vector.quantize_mx(out=y_codes[:].bitcast(FP8X4), scales=y_scales[:, cols], in_=yb[:])
+            nc.sync.dma_start(out=out_words[:, cols], in_=y_codes[:].bitcast(I32))
+
+        gather(0)
+        gather(1)
+        for pos in range(E):
+            first_layer(pos)
+            if pos == 0:
+                w2raw["cold"] = shared.tile([P, COLD * N * 2], U8, name="w2c_raw", align_bytes=64, offset=0)
+                nc.sync.dma_start(out=w2raw["cold"][:].bitcast(I32).rearrange("p (f w) -> p f w", f=COLD),
+                                  in_=w2c_words.rearrange("f s p c -> p (f s) c").bitcast(I32))
+            if pos == 1:
+                w2raw["hot"] = shared.tile([P, N], U32, name="w2h_raw", align_bytes=64, offset=REGION)
+                nc.sync.dma_start(out=w2raw["hot"][:].bitcast(I32),
+                                  in_=w2h_words[0, 0].rearrange("p n d -> p (n d)").bitcast(I32))
+            if pos + 2 < E:
+                load_w1(pos + 2)
+            deal_w2(pos)
+            quantise_h(pos)
+            if pos + 2 < E:
+                gather(pos + 2)
+            for j0, n in pieces(pos):
+                second_layer(pos, j0, n)
+        done = [(pos, j0, n) for pos in range(E) for j0, n in pieces(pos)]
+        for i, (pos, j0, n) in enumerate(done):
+            planes(pos, j0, n, i % 2)
+        for q in range(4):
+            nc.sync.dma_start(out=out_2[0, 4 * q : 4 * q + 4, :].bitcast(I32), in_=y_scales[32 * q : 32 * q + 4, :].bitcast(I32))

@@ -16,16 +16,22 @@ U8 = mybir.dt.uint8
 FP8X4 = mybir.dt.float8_e4m3fn_x4
 FP4X4 = mybir.dt.float4_e2m1fn_x4
 ACT = mybir.ActivationFunctionType
+ALU = mybir.AluOpType
 
 P = 128
 PACK = 4
 PASSES = K // (P * PACK)
 COLD = E - 1
+T_WIDE = 704
+V_RELU = ()
+V_YEV = ((3,0,0),(4,0,0),(0,0,0))
+
 ORDER = [1, 2, 3, 4, 0]
-REGION = 4096
-BANK = 2048
-W1_BASE = (E + 2) * REGION
-W1_COLD_BYTES = PASSES * H * 2
+AT_GW = [0, 0, 0, 24576, 28672]
+AT_XS = 9152
+AT_LATE = 9792
+AT_HB = [24576, 28672, 32768, 36864, 53248]
+AT_W1 = 65536
 
 
 def load_scale_rows(queue, tile, rows):
@@ -48,14 +54,17 @@ def tile_moe_hot_s_mlp_relu2_kernel(
         shared = ctx.enter_context(tc.tile_pool(name="shared", bufs=1))
         ring = ctx.enter_context(tc.tile_pool(name="ring", bufs=6))
         psum1 = ctx.enter_context(tc.psum_pool(name="psum1", bufs=1))
-        psum2 = ctx.enter_context(tc.psum_pool(name="psum2", bufs=4))
+        psum2 = ctx.enter_context(tc.psum_pool(name="psum2", bufs=3))
 
         offsets = lists.tile([P, S // 16], U16, name="offsets")
         nc.sync.dma_start(offsets[:], offs)
 
-        xs = keep.tile([P, PASSES * T], U8, name="xs", align_bytes=64)
+        xs = shared.tile([P, T_WIDE], U8, name="xs", align_bytes=64, offset=AT_XS)
         nc.vector.memset(xs[:].bitcast(I32), 0)
-        load_scale_rows(nc.scalar, xs, x_scales)
+        groups = x_scales.rearrange("s (q r) t -> (s q) r t", r=4).bitcast(I32)
+        for rows, src in ((xs[0:8, :T], groups[0:12:11]), (xs[32:36, :T], groups[1]), (xs[64:68, :T], groups[2]),
+                          (xs[96:128, :T], groups[3:11].rearrange("g r t -> (g r) t"))):
+            nc.scalar.dma_start(out=rows.bitcast(I32), in_=src)
 
         xw = keep.tile([P, PASSES * T], U32, name="xw", align_bytes=64)
         nc.sync.dma_start(
@@ -63,160 +72,168 @@ def tile_moe_hot_s_mlp_relu2_kernel(
             in_=x_words.rearrange("s p t d -> p s (t d)").bitcast(I32),
         )
 
-        w1 = {}
+        w1, gw, hb, hq, ysb, w2, w2s = {}, {}, {}, {}, {}, {}, {}
 
-        def load_w1(pos):
-            e = ORDER[pos]
-            if e == 0:
-                t = shared.tile([P, PASSES * H * 4], U8, name="w1_hot", align_bytes=64, offset=W1_BASE + W1_COLD_BYTES)
-                src = w1h_words[0].rearrange("s p i d -> p s (i d)")
-            else:
-                t = shared.tile([P, W1_COLD_BYTES], U8, name="w1_cold%d" % pos, align_bytes=64,
-                                offset=W1_BASE + W1_COLD_BYTES * ((pos + 1) % 2))
-                src = w1c_words[e - 1].rearrange("s p c -> p s c")
-            nc.sync.dma_start(out=t[:].bitcast(I32).rearrange("p (s w) -> p s w", s=PASSES), in_=src.bitcast(I32))
-            w1[pos] = t
-
-        load_w1(0)
+        first = shared.tile([P, 2 * PASSES * H * 2], U8, name="w1_first", align_bytes=64, offset=AT_W1)
+        nc.sync.dma_start(out=first[:].bitcast(I32).rearrange("p (a w) -> p a w", a=2 * PASSES),
+                          in_=w1c_words[0:2].rearrange("f s p c -> p (f s) c").bitcast(I32))
+        for f in range(2):
+            w1[1 + f] = first[:, f * PASSES * H * 2 : (f + 1) * PASSES * H * 2]
         w1cs = keep.tile([P, COLD * PASSES * H], U8, name="w1cs", align_bytes=64)
         nc.vector.memset(w1cs[:].bitcast(I32), 0)
-        load_scale_rows(nc.sync, w1cs, w1c_scales.rearrange("f s b i -> (f s) b i"))
-        load_w1(1)
-
-        w2cs_raw = keep.tile([P, COLD * N], U8, name="w2cs_raw", align_bytes=64)
-        nc.gpsimd.memset(w2cs_raw[:].bitcast(I32), 0)
-        load_scale_rows(nc.sync, w2cs_raw, w2c_scales.rearrange("f s b i -> (f s) b i"))
-        w2hs_raw = keep.tile([P, N], U8, name="w2hs_raw", align_bytes=64)
-        nc.gpsimd.memset(w2hs_raw[:].bitcast(I32), 0)
-        w1hs = keep.tile([P, PASSES * H], U8, name="w1hs", align_bytes=64)
-        nc.gpsimd.memset(w1hs[:].bitcast(I32), 0)
-        load_scale_rows(nc.sync, w1hs, w1h_scales[0])
-        load_scale_rows(nc.sync, w2hs_raw, w2h_scales[0])
+        load_scale_rows(nc.gpsimd, w1cs, w1c_scales.rearrange("f s b i -> (f s) b i"))
         ident = keep.tile([P, P], F32, name="ident")
         make_identity(nc, ident[:])
+        moved = keep.tile([P, (PASSES - 1) * S], U8, name="moved", align_bytes=64)
+        nc.vector.memset(moved[:].bitcast(I32), 0)
 
         y_scales = keep.tile([P, S], U8, name="y_scales", align_bytes=64)
         out_rows = out_0.rearrange("(p t) j -> p t j", t=PACK)
         out_words = out_1[0].rearrange("p j d -> p (j d)").bitcast(I32)
 
-        gw, gs, hb, hq, ysb, w2raw, w2, w2s = {}, {}, {}, {}, {}, {}, {}, {}
+        gs = keep.tile([P, S], U8, name="gs", align_bytes=64)
+        for j0 in range(0, S, 2 * C):
+            j1 = min(j0 + 2 * C, S)
+            nc.vector.tensor_copy(out=gs[:, j0:j1], in_=xs[:].indirect(offsets[:, j0 // 16 : j1 // 16]))
+        for s in range(1, PASSES):
+            for q in range(4):
+                g = 4 * s + q
+                row = 4 if g == 11 else 96 + 4 * (g - 3)
+                nc.sync.dma_start(out=moved[32 * q : 32 * q + 4, (s - 1) * S : s * S].bitcast(I32),
+                                  in_=gs[row : row + 4, :].bitcast(I32))
 
-        def pieces(pos):
-            return [(0, P), (P, P)] if pos == E - 1 else [(0, C)]
+        second = shared.tile([P, 12288], U8, name="second", align_bytes=64, offset=AT_LATE)
+        w2cs_raw, w2c_raw = second[:, :2048], second[:, 2048:6144]
+        nc.gpsimd.memset(w2cs_raw.bitcast(I32), 0)
+        load_scale_rows(nc.sync, w2cs_raw, w2c_scales.rearrange("f s b i -> (f s) b i"))
+        nc.sync.dma_start(out=w2c_raw.bitcast(I32).rearrange("p (f w) -> p f w", f=COLD),
+                          in_=w2c_words.rearrange("f s p c -> p (f s) c").bitcast(I32))
+        for f in range(2, COLD):
+            w1[1 + f] = second[:, f * 3072 : (f + 1) * 3072]
+            nc.sync.dma_start(out=w1[1 + f].bitcast(I32).rearrange("p (s w) -> p s w", s=PASSES),
+                              in_=w1c_words[f].rearrange("s p c -> p s c").bitcast(I32))
+        late = {}
+        pair = shared.tile([P, 3 * PASSES * C], U32, name="gw_first", align_bytes=64, offset=0)
 
-        def gather(pos):
-            e = ORDER[pos]
-            gs[pos] = shared.tile([P, PASSES * C], U8, name="gs%d" % pos, align_bytes=64, offset=pos * REGION)
-            gw[pos] = shared.tile([P, PASSES * C], U32, name="gw%d" % pos, align_bytes=64, offset=pos * REGION + 1024)
+        def pieces(e):
+            return [(0, P), (P, P)] if e == ORDER[-1] else [(0, C)]
+
+        def gather(e):
+            pos = ORDER.index(e)
+            if pos < 3:
+                gw[e] = pair[:, pos * PASSES * C : (pos + 1) * PASSES * C]
+            else:
+                gw[e] = shared.tile([P, PASSES * C], U32, name="gw%d" % e, align_bytes=64, offset=AT_GW[pos])
             idx = offsets[:, e * C // 16 : (e + 1) * C // 16]
             for s in range(PASSES):
-                nc.vector.tensor_copy(out=gs[pos][:, s * C : (s + 1) * C], in_=xs[:, s * T : (s + 1) * T].indirect(idx))
-            for j0, n in pieces(pos):
-                idx = offsets[:, (e * C + j0) // 16 : (e * C + j0 + n) // 16]
-                for s in range(PASSES):
-                    nc.vector.tensor_copy(out=gw[pos][:, s * C + j0 : s * C + j0 + n],
-                                          in_=xw[:, s * T : (s + 1) * T].indirect(idx))
+                nc.vector.tensor_copy(out=gw[e][:, s * C : (s + 1) * C], in_=xw[:, s * T : (s + 1) * T].indirect(idx))
 
-        def first_layer(pos):
-            e = ORDER[pos]
-            hb[pos] = shared.tile([P, C * PACK], BF16, name="hb%d" % pos, align_bytes=64, offset=(pos + 2) * REGION)
+        def token_scales(e, s, half):
+            j0 = e * C + half * P
+            if s == 0:
+                return gs[:, j0 : j0 + P]
+            return moved[:, (s - 1) * S + j0 : (s - 1) * S + j0 + P]
+
+        def first_layer(e):
+            hb[e] = shared.tile([P, C * PACK], BF16, name="hb%d" % e, align_bytes=64, offset=AT_HB[ORDER.index(e)])
+            accs = [psum1.tile([P, H], F32, name="acc1", bufs=3)[:] for half in range(C // P)]
+            for half, s in [(half, s) for half in range(C // P) for s in range(PASSES)]:
+                cols = slice(s * C + half * P, s * C + (half + 1) * P)
+                if e == 0:
+                    rhs = w1[e][:, s * H * 4 : (s + 1) * H * 4].bitcast(FP8X4)
+                    rhs_scale = late["w1hs"][:, s * H : (s + 1) * H]
+                else:
+                    rhs = w1[e][:, s * H * 2 : (s + 1) * H * 2].bitcast(FP4X4)
+                    a = (e - 1) * PASSES + s
+                    rhs_scale = w1cs[:, a * H : (a + 1) * H]
+                nc.tensor.matmul_mx(out=accs[half], lhsT=gw[e][:, cols].bitcast(FP8X4), lhsT_scale=token_scales(e, s, half),
+                                    rhs=rhs, rhs_scale=rhs_scale, start=(s == 0), stop=(s == PASSES - 1))
             for half in range(C // P):
-                acc = psum1.tile([P, H], F32, name="acc1_%d_%d" % (pos, half), offset=BANK * ((pos + half) % 3))
-                for s in range(PASSES):
-                    cols = slice(s * C + half * P, s * C + (half + 1) * P)
-                    if e == 0:
-                        rhs = w1[pos][:, s * H * 4 : (s + 1) * H * 4].bitcast(FP8X4)
-                        rhs_scale = w1hs[:, s * H : (s + 1) * H]
-                    else:
-                        rhs = w1[pos][:, s * H * 2 : (s + 1) * H * 2].bitcast(FP4X4)
-                        a = (e - 1) * PASSES + s
-                        rhs_scale = w1cs[:, a * H : (a + 1) * H]
-                    nc.tensor.matmul_mx(out=acc[:], lhsT=gw[pos][:, cols].bitcast(FP8X4), lhsT_scale=gs[pos][:, cols],
-                                        rhs=rhs, rhs_scale=rhs_scale, start=(s == 0), stop=(s == PASSES - 1))
                 relu = ring.tile([P, PACK, P], F32, name="relu")
-                nc.scalar.activation(out=relu[:], in_=acc[:].rearrange("j (m t) -> j t m", t=PACK), func=ACT.Relu)
-                turned = psum1.tile([P, PACK, P], F32, name="turned_%d_%d" % (pos, half),
-                                    offset=BANK * ((pos + 2) % 3 if half == 0 else 3))
+                src = accs[half].rearrange("j (m t) -> j t m", t=PACK)
+                if (e, half) in V_RELU:
+                    nc.vector.tensor_scalar_max(out=relu[:], in0=src, scalar1=0.0)
+                else:
+                    nc.scalar.activation(out=relu[:], in_=src, func=ACT.Relu)
+                turned = psum1.tile([P, PACK, P], F32, name="turned", bufs=2)
                 for t in range(PACK):
                     nc.tensor.transpose(turned[:, t, :], relu[:, t, :], ident[:])
                 nc.scalar.activation(
-                    out=hb[pos][:, half * P * PACK : (half + 1) * P * PACK].rearrange("m (j t) -> m j t", t=PACK),
+                    out=hb[e][:, half * P * PACK : (half + 1) * P * PACK].rearrange("m (j t) -> m j t", t=PACK),
                     in_=turned[:].rearrange("m t j -> m j t"), func=ACT.Square)
 
-        def quantise_h(pos):
-            for j0, n in pieces(pos):
+        def quantise_h(e):
+            for j0, n in pieces(e):
                 codes = ring.tile([P, n], U32, name="h_codes", align_bytes=64)
                 scales = ring.tile([P, n], U8, name="h_scales", align_bytes=64)
-                nc.vector.quantize_mx(out=codes[:].bitcast(FP8X4), scales=scales[:], in_=hb[pos][:, j0 * PACK : (j0 + n) * PACK])
-                hq[pos, j0] = (codes, scales)
+                nc.vector.quantize_mx(out=codes[:].bitcast(FP8X4), scales=scales[:], in_=hb[e][:, j0 * PACK : (j0 + n) * PACK])
+                hq[e, j0] = (codes, scales)
 
-        def deal_w2(pos):
-            e = ORDER[pos]
-            w2s[pos] = keep.tile([P, N], U8, name="w2s%d" % pos, align_bytes=64)
-            raw = w2hs_raw[:] if e == 0 else w2cs_raw[:, (e - 1) * N : e * N]
-            nc.gpsimd.tensor_copy(out=w2s[pos][:].rearrange("p (t m) -> p t m", t=PACK),
-                                  in_=raw.rearrange("p (m t) -> p t m", t=PACK))
-            if e == 0:
-                w2[pos] = keep.tile([P, N], U32, name="w2_%d" % pos, align_bytes=64)
-                nc.scalar.copy(out=w2[pos][:].rearrange("p (t m) -> p t m", t=PACK),
-                               in_=w2raw["hot"][:].rearrange("p (m t) -> p t m", t=PACK))
-            else:
-                w2[pos] = keep.tile([P, N * 2], U8, name="w2_%d" % pos, align_bytes=64)
-                wc = slice((e - 1) * N * 2, e * N * 2)
-                nc.scalar.copy(out=w2[pos][:].bitcast(U16).rearrange("p (t m) -> p t m", t=PACK),
-                               in_=w2raw["cold"][:, wc].bitcast(U16).rearrange("p (m t) -> p t m", t=PACK))
+        def deal_w2(e, words, scales):
+            w2s[e] = keep.tile([P, N], U8, name="w2s%d" % e, align_bytes=64)
+            nc.vector.tensor_copy(out=w2s[e][:].rearrange("p (t m) -> p t m", t=PACK),
+                                  in_=scales.rearrange("p (m t) -> p t m", t=PACK))
+            w2[e] = keep.tile([P, N * (4 if e == 0 else 2)], U8, name="w2_%d" % e, align_bytes=64)
+            word = U32 if e == 0 else U16
+            (nc.vector.tensor_copy if e in (0,1,2,3,4) else nc.scalar.copy)(out=w2[e][:].bitcast(word).rearrange("p (t m) -> p t m", t=PACK),
+                           in_=words.bitcast(word).rearrange("p (m t) -> p t m", t=PACK))
 
-        def second_layer(pos, j0, n):
-            e = ORDER[pos]
-            codes, scales = hq[pos, j0]
-            ysb[pos, j0] = ring.tile([P, PACK, n], F32, name="ysb")
+        def second_layer(e, j0, n):
+            codes, scales = hq[e, j0]
+            ysb[e, j0] = ring.tile([P, PACK, n], F32, name="ysb")
             per_bank = N // n
             for t0 in range(0, PACK, per_bank):
                 acc = psum2.tile([P, per_bank, n], F32, name="acc2")
                 for u in range(per_bank):
                     t = t0 + u
                     if e == 0:
-                        lhsT = w2[pos][:, t * P : (t + 1) * P].bitcast(FP8X4)
+                        lhsT = w2[e][:, 4 * t * P : 4 * (t + 1) * P].bitcast(FP8X4)
                     else:
-                        lhsT = w2[pos][:, 2 * t * P : 2 * (t + 1) * P].bitcast(FP4X4)
-                    nc.tensor.matmul_mx(out=acc[:, u, :], lhsT=lhsT, lhsT_scale=w2s[pos][:, t * P : (t + 1) * P],
+                        lhsT = w2[e][:, 2 * t * P : 2 * (t + 1) * P].bitcast(FP4X4)
+                    nc.tensor.matmul_mx(out=acc[:, u, :], lhsT=lhsT, lhsT_scale=w2s[e][:, t * P : (t + 1) * P],
                                         rhs=codes[:].bitcast(FP8X4), rhs_scale=scales[:], start=True, stop=True)
-                nc.scalar.copy(out=ysb[pos, j0][:, t0 : t0 + per_bank, :], in_=acc[:])
-            nc.sync.dma_start(out=out_rows[:, :, e * C + j0 : e * C + j0 + n], in_=ysb[pos, j0][:])
+                if (e, j0, t0) in V_YEV:
+                    nc.vector.tensor_copy(out=ysb[e, j0][:, t0 : t0 + per_bank, :], in_=acc[:])
+                else:
+                    nc.scalar.copy(out=ysb[e, j0][:, t0 : t0 + per_bank, :], in_=acc[:])
+            nc.sync.dma_start(out=out_rows[:, :, e * C + j0 : e * C + j0 + n], in_=ysb[e, j0][:])
 
-        def planes(pos, j0, n, slot):
-            e = ORDER[pos]
+        def planes(e, j0, n):
             cols = slice(e * C + j0, e * C + j0 + n)
-            yb = shared.tile([P, n * PACK], BF16, name="yb%d_%d" % (pos, j0), align_bytes=64,
-                             offset=(E - 1) * REGION + 2048 * slot)
+            yb = ring.tile([P, n * PACK], BF16, name="yb", align_bytes=64)
             nc.vector.tensor_copy(out=yb[:].rearrange("p (c i t) -> p c t i", i=4, t=PACK),
-                                  in_=ysb[pos, j0][:].rearrange("p t (c i) -> p c t i", i=4))
+                                  in_=ysb[e, j0][:].rearrange("p t (c i) -> p c t i", i=4))
             y_codes = ring.tile([P, n], U32, name="y_codes", align_bytes=64)
             nc.vector.quantize_mx(out=y_codes[:].bitcast(FP8X4), scales=y_scales[:, cols], in_=yb[:])
             nc.sync.dma_start(out=out_words[:, cols], in_=y_codes[:].bitcast(I32))
 
-        gather(0)
-        gather(1)
-        for pos in range(E):
-            first_layer(pos)
-            if pos == 0:
-                w2raw["cold"] = shared.tile([P, COLD * N * 2], U8, name="w2c_raw", align_bytes=64, offset=0)
-                nc.sync.dma_start(out=w2raw["cold"][:].bitcast(I32).rearrange("p (f w) -> p f w", f=COLD),
-                                  in_=w2c_words.rearrange("f s p c -> p (f s) c").bitcast(I32))
+        gather(ORDER[0])
+        gather(ORDER[1])
+        gather(ORDER[2])
+        for pos, e in enumerate(ORDER):
+            first_layer(e)
             if pos == 1:
-                w2raw["hot"] = shared.tile([P, N], U32, name="w2h_raw", align_bytes=64, offset=REGION)
-                nc.sync.dma_start(out=w2raw["hot"][:].bitcast(I32),
-                                  in_=w2h_words[0, 0].rearrange("p n d -> p (n d)").bitcast(I32))
-            if pos + 2 < E:
-                load_w1(pos + 2)
-            deal_w2(pos)
-            quantise_h(pos)
-            if pos + 2 < E:
-                gather(pos + 2)
-            for j0, n in pieces(pos):
-                second_layer(pos, j0, n)
-        done = [(pos, j0, n) for pos in range(E) for j0, n in pieces(pos)]
-        for i, (pos, j0, n) in enumerate(done):
-            planes(pos, j0, n, i % 2)
+                w1[0] = shared.tile([P, PASSES * H * 4], U8, name="w1h", align_bytes=64, offset=AT_W1 - 6144 + 64)
+                nc.sync.dma_start(out=w1[0][:].bitcast(I32).rearrange("p (s w) -> p s w", s=PASSES),
+                                  in_=w1h_words[0].rearrange("s p i d -> p s (i d)").bitcast(I32))
+                late["w1hs"] = shared.tile([P, PASSES * H], U8, name="w1hs", align_bytes=64, offset=AT_W1 + 6144 - 576 - 1536)
+                nc.gpsimd.memset(late["w1hs"][:].bitcast(I32), 0)
+                load_scale_rows(nc.sync, late["w1hs"], w1h_scales[0])
+                w2hs_raw = shared.tile([P, N], U8, name="w2hs_raw", align_bytes=64, offset=AT_W1 + 6144 - 576)
+                nc.gpsimd.memset(w2hs_raw[:].bitcast(I32), 0)
+                load_scale_rows(nc.sync, w2hs_raw, w2h_scales[0])
+                w2h_raw = shared.tile([P, N * 4], U8, name="w2h_raw", align_bytes=64, offset=AT_W1 + 6144 - 64)
+                nc.sync.dma_start(out=w2h_raw[:].bitcast(I32), in_=w2h_words[0, 0].rearrange("p n d -> p (n d)").bitcast(I32))
+            if e == 0:
+                deal_w2(e, w2h_raw[:], w2hs_raw[:])
+            else:
+                deal_w2(e, w2c_raw[:, (e - 1) * N * 2 : e * N * 2], w2cs_raw[:, (e - 1) * N : e * N])
+            quantise_h(e)
+            if pos + 3 < E:
+                gather(ORDER[pos + 3])
+            for j0, n in pieces(e):
+                second_layer(e, j0, n)
+                planes(e, j0, n)
         for q in range(4):
-            nc.sync.dma_start(out=out_2[0, 4 * q : 4 * q + 4, :].bitcast(I32), in_=y_scales[32 * q : 32 * q + 4, :].bitcast(I32))
+            queue = nc.scalar if q % 2 == 0 else nc.sync
+            queue.dma_start(out=out_2[0, 4 * q : 4 * q + 4, :].bitcast(I32), in_=y_scales[32 * q : 32 * q + 4, :].bitcast(I32))

@@ -34,10 +34,10 @@ AT_HB = [24576, 28672, 32768, 36864, 53248]
 AT_W1 = 65536
 
 
-def load_scale_rows(queue, tile, rows):
+def load_scale_rows(queues, tile, rows):
     planes = rows.shape[0]
     for q in range(4):
-        queue.dma_start(
+        queues[q % len(queues)].dma_start(
             out=tile[32 * q : 32 * q + 4, :].bitcast(I32).rearrange("r (a w) -> r a w", a=planes),
             in_=rows[:, 4 * q : 4 * q + 4, :].bitcast(I32).rearrange("a r w -> r a w"),
         )
@@ -81,7 +81,7 @@ def tile_moe_hot_s_mlp_relu2_kernel(
             w1[1 + f] = first[:, f * PASSES * H * 2 : (f + 1) * PASSES * H * 2]
         w1cs = keep.tile([P, COLD * PASSES * H], U8, name="w1cs", align_bytes=64)
         nc.vector.memset(w1cs[:].bitcast(I32), 0)
-        load_scale_rows(nc.gpsimd, w1cs, w1c_scales.rearrange("f s b i -> (f s) b i"))
+        load_scale_rows([nc.scalar, nc.gpsimd], w1cs, w1c_scales.rearrange("f s b i -> (f s) b i"))
         ident = keep.tile([P, P], F32, name="ident")
         make_identity(nc, ident[:])
         moved = keep.tile([P, (PASSES - 1) * S], U8, name="moved", align_bytes=64)
@@ -102,16 +102,6 @@ def tile_moe_hot_s_mlp_relu2_kernel(
                 nc.sync.dma_start(out=moved[32 * q : 32 * q + 4, (s - 1) * S : s * S].bitcast(I32),
                                   in_=gs[row : row + 4, :].bitcast(I32))
 
-        second = shared.tile([P, 12288], U8, name="second", align_bytes=64, offset=AT_LATE)
-        w2cs_raw, w2c_raw = second[:, :2048], second[:, 2048:6144]
-        nc.gpsimd.memset(w2cs_raw.bitcast(I32), 0)
-        load_scale_rows(nc.sync, w2cs_raw, w2c_scales.rearrange("f s b i -> (f s) b i"))
-        nc.sync.dma_start(out=w2c_raw.bitcast(I32).rearrange("p (f w) -> p f w", f=COLD),
-                          in_=w2c_words.rearrange("f s p c -> p (f s) c").bitcast(I32))
-        for f in range(2, COLD):
-            w1[1 + f] = second[:, f * 3072 : (f + 1) * 3072]
-            nc.sync.dma_start(out=w1[1 + f].bitcast(I32).rearrange("p (s w) -> p s w", s=PASSES),
-                              in_=w1c_words[f].rearrange("s p c -> p s c").bitcast(I32))
         late = {}
         pair = shared.tile([P, 3 * PASSES * C], U32, name="gw_first", align_bytes=64, offset=0)
 
@@ -158,6 +148,11 @@ def tile_moe_hot_s_mlp_relu2_kernel(
                 turned = psum1.tile([P, PACK, P], F32, name="turned", bufs=2)
                 for t in range(PACK):
                     nc.tensor.transpose(turned[:, t, :], relu[:, t, :], ident[:])
+                late[e, half] = turned
+
+        def square(e):
+            for half in range(C // P):
+                turned = late[e, half]
                 nc.scalar.activation(
                     out=hb[e][:, half * P * PACK : (half + 1) * P * PACK].rearrange("m (j t) -> m j t", t=PACK),
                     in_=turned[:].rearrange("m t j -> m j t"), func=ACT.Square)
@@ -207,21 +202,39 @@ def tile_moe_hot_s_mlp_relu2_kernel(
             nc.vector.quantize_mx(out=y_codes[:].bitcast(FP8X4), scales=y_scales[:, cols], in_=yb[:])
             nc.sync.dma_start(out=out_words[:, cols], in_=y_codes[:].bitcast(I32))
 
+        def finish(e):
+            for j0, n in pieces(e):
+                second_layer(e, j0, n)
+                planes(e, j0, n)
+
         gather(ORDER[0])
+        second = shared.tile([P, 12288], U8, name="second", align_bytes=64, offset=AT_LATE)
+        w2cs_raw, w2c_raw = second[:, :2048], second[:, 2048:6144]
+        nc.vector.memset(w2cs_raw.bitcast(I32), 0)
+        load_scale_rows([nc.sync], w2cs_raw, w2c_scales.rearrange("f s b i -> (f s) b i"))
+        nc.sync.dma_start(out=w2c_raw.bitcast(I32).rearrange("p (f w) -> p f w", f=COLD),
+                          in_=w2c_words.rearrange("f s p c -> p (f s) c").bitcast(I32))
+        for f in range(2, COLD):
+            w1[1 + f] = second[:, f * 3072 : (f + 1) * 3072]
+            nc.sync.dma_start(out=w1[1 + f].bitcast(I32).rearrange("p (s w) -> p s w", s=PASSES),
+                              in_=w1c_words[f].rearrange("s p c -> p s c").bitcast(I32))
         gather(ORDER[1])
         gather(ORDER[2])
         for pos, e in enumerate(ORDER):
             first_layer(e)
+            if pos >= 1:
+                finish(ORDER[pos - 1])
+            square(e)
             if pos == 1:
                 w1[0] = shared.tile([P, PASSES * H * 4], U8, name="w1h", align_bytes=64, offset=AT_W1 - 6144 + 64)
                 nc.sync.dma_start(out=w1[0][:].bitcast(I32).rearrange("p (s w) -> p s w", s=PASSES),
                                   in_=w1h_words[0].rearrange("s p i d -> p s (i d)").bitcast(I32))
                 late["w1hs"] = shared.tile([P, PASSES * H], U8, name="w1hs", align_bytes=64, offset=AT_W1 + 6144 - 576 - 1536)
-                nc.gpsimd.memset(late["w1hs"][:].bitcast(I32), 0)
-                load_scale_rows(nc.sync, late["w1hs"], w1h_scales[0])
+                nc.vector.memset(late["w1hs"][:].bitcast(I32), 0)
+                load_scale_rows([nc.sync], late["w1hs"], w1h_scales[0])
                 w2hs_raw = shared.tile([P, N], U8, name="w2hs_raw", align_bytes=64, offset=AT_W1 + 6144 - 576)
-                nc.gpsimd.memset(w2hs_raw[:].bitcast(I32), 0)
-                load_scale_rows(nc.sync, w2hs_raw, w2h_scales[0])
+                nc.vector.memset(w2hs_raw[:].bitcast(I32), 0)
+                load_scale_rows([nc.sync], w2hs_raw, w2h_scales[0])
                 w2h_raw = shared.tile([P, N * 4], U8, name="w2h_raw", align_bytes=64, offset=AT_W1 + 6144 - 64)
                 nc.sync.dma_start(out=w2h_raw[:].bitcast(I32), in_=w2h_words[0, 0].rearrange("p n d -> p (n d)").bitcast(I32))
             if e == 0:
@@ -231,9 +244,8 @@ def tile_moe_hot_s_mlp_relu2_kernel(
             quantise_h(e)
             if pos + 3 < E:
                 gather(ORDER[pos + 3])
-            for j0, n in pieces(e):
-                second_layer(e, j0, n)
-                planes(e, j0, n)
+        for e in ORDER[E - 1 :]:
+            finish(e)
         for q in range(4):
             queue = nc.scalar if q % 2 == 0 else nc.sync
             queue.dma_start(out=out_2[0, 4 * q : 4 * q + 4, :].bitcast(I32), in_=y_scales[32 * q : 32 * q + 4, :].bitcast(I32))

from contextlib import ExitStack

import concourse.mybir as mybir
from concourse.masks import make_identity

K, T, E, C, H, N = 1536, 640, 5, 256, 512, 512
S = E * C
FLOPS = 2 * S * (K * H + H * N)

F32 = mybir.dt.float32
BF16 = mybir.dt.bfloat16
I32 = mybir.dt.int32
U32 = mybir.dt.uint32
U16 = mybir.dt.uint16
U8 = mybir.dt.uint8
FP8X4 = mybir.dt.float8_e4m3fn_x4
FP4X4 = mybir.dt.float4_e2m1fn_x4
ACT = mybir.ActivationFunctionType
ALU = mybir.AluOpType

P = 128
PACK = 4
PASSES = K // (P * PACK)
COLD = E - 1
T_WIDE = 704
V_RELU = ()
V_YEV = ((3,0,0),(4,0,0),(0,0,0))

ORDER = [1, 2, 3, 4, 0]
AT_GW = [0, 0, 0, 24576, 28672]
AT_XS = 9152
AT_LATE = 9792
AT_HB = [24576, 28672, 32768, 36864, 53248]
AT_W1 = 65536


def load_scale_rows(queues, tile, rows):
    planes = rows.shape[0]
    for q in range(4):
        queues[q % len(queues)].dma_start(
            out=tile[32 * q : 32 * q + 4, :].bitcast(I32).rearrange("r (a w) -> r a w", a=planes),
            in_=rows[:, 4 * q : 4 * q + 4, :].bitcast(I32).rearrange("a r w -> r a w"),
        )


def tile_moe_hot_s_mlp_relu2_kernel(
    tc, x_words, x_scales, w1h_words, w1h_scales, w2h_words, w2h_scales, w1c_words, w1c_scales, w2c_words, w2c_scales, offs,
    out_0, out_1, out_2,
):
    nc = tc.nc
    with ExitStack() as ctx:
        lists = ctx.enter_context(tc.tile_pool(name="lists", bufs=1))
        keep = ctx.enter_context(tc.tile_pool(name="keep", bufs=1))
        shared = ctx.enter_context(tc.tile_pool(name="shared", bufs=1))
        ring = ctx.enter_context(tc.tile_pool(name="ring", bufs=6))
        psum1 = ctx.enter_context(tc.psum_pool(name="psum1", bufs=1))
        psum2 = ctx.enter_context(tc.psum_pool(name="psum2", bufs=3))

        offsets = lists.tile([P, S // 16], U16, name="offsets")
        nc.sync.dma_start(offsets[:], offs)

        xs = shared.tile([P, T_WIDE], U8, name="xs", align_bytes=64, offset=AT_XS)
        nc.vector.memset(xs[:].bitcast(I32), 0)
        groups = x_scales.rearrange("s (q r) t -> (s q) r t", r=4).bitcast(I32)
        for rows, src in ((xs[0:8, :T], groups[0:12:11]), (xs[32:36, :T], groups[1]), (xs[64:68, :T], groups[2]),
                          (xs[96:128, :T], groups[3:11].rearrange("g r t -> (g r) t"))):
            nc.scalar.dma_start(out=rows.bitcast(I32), in_=src)

        xw = keep.tile([P, PASSES * T], U32, name="xw", align_bytes=64)
        nc.sync.dma_start(
            out=xw[:].bitcast(I32).rearrange("p (s t) -> p s t", s=PASSES),
            in_=x_words.rearrange("s p t d -> p s (t d)").bitcast(I32),
        )

        w1, gw, hb, hq, ysb, w2, w2s = {}, {}, {}, {}, {}, {}, {}

        first = shared.tile([P, 2 * PASSES * H * 2], U8, name="w1_first", align_bytes=64, offset=AT_W1)
        nc.sync.dma_start(out=first[:].bitcast(I32).rearrange("p (a w) -> p a w", a=2 * PASSES),
                          in_=w1c_words[0:2].rearrange("f s p c -> p (f s) c").bitcast(I32))
        for f in range(2):
            w1[1 + f] = first[:, f * PASSES * H * 2 : (f + 1) * PASSES * H * 2]
        w1cs = keep.tile([P, COLD * PASSES * H], U8, name="w1cs", align_bytes=64)
        nc.vector.memset(w1cs[:].bitcast(I32), 0)
        load_scale_rows([nc.scalar, nc.gpsimd], w1cs, w1c_scales.rearrange("f s b i -> (f s) b i"))
        ident = keep.tile([P, P], F32, name="ident")
        make_identity(nc, ident[:])
        moved = keep.tile([P, (PASSES - 1) * S], U8, name="moved", align_bytes=64)
        nc.vector.memset(moved[:].bitcast(I32), 0)

        y_scales = keep.tile([P, S], U8, name="y_scales", align_bytes=64)
        out_rows = out_0.rearrange("(p t) j -> p t j", t=PACK)
        out_words = out_1[0].rearrange("p j d -> p (j d)").bitcast(I32)

        gs = keep.tile([P, S], U8, name="gs", align_bytes=64)
        for j0 in range(0, S, 2 * C):
            j1 = min(j0 + 2 * C, S)
            nc.vector.tensor_copy(out=gs[:, j0:j1], in_=xs[:].indirect(offsets[:, j0 // 16 : j1 // 16]))
        for s in range(1, PASSES):
            for q in range(4):
                g = 4 * s + q
                row = 4 if g == 11 else 96 + 4 * (g - 3)
                nc.sync.dma_start(out=moved[32 * q : 32 * q + 4, (s - 1) * S : s * S].bitcast(I32),
                                  in_=gs[row : row + 4, :].bitcast(I32))

        late = {}
        pair = shared.tile([P, 3 * PASSES * C], U32, name="gw_first", align_bytes=64, offset=0)

        def pieces(e):
            return [(0, P), (P, P)] if e == ORDER[-1] else [(0, C)]

        def gather(e):
            pos = ORDER.index(e)
            if pos < 3:
                gw[e] = pair[:, pos * PASSES * C : (pos + 1) * PASSES * C]
            else:
                gw[e] = shared.tile([P, PASSES * C], U32, name="gw%d" % e, align_bytes=64, offset=AT_GW[pos])
            idx = offsets[:, e * C // 16 : (e + 1) * C // 16]
            for s in range(PASSES):
                nc.vector.tensor_copy(out=gw[e][:, s * C : (s + 1) * C], in_=xw[:, s * T : (s + 1) * T].indirect(idx))

        def token_scales(e, s, half):
            j0 = e * C + half * P
            if s == 0:
                return gs[:, j0 : j0 + P]
            return moved[:, (s - 1) * S + j0 : (s - 1) * S + j0 + P]

        def first_layer(e):
            hb[e] = shared.tile([P, C * PACK], BF16, name="hb%d" % e, align_bytes=64, offset=AT_HB[ORDER.index(e)])
            accs = [psum1.tile([P, H], F32, name="acc1", bufs=3)[:] for half in range(C // P)]
            for half, s in [(half, s) for half in range(C // P) for s in range(PASSES)]:
                cols = slice(s * C + half * P, s * C + (half + 1) * P)
                if e == 0:
                    rhs = w1[e][:, s * H * 4 : (s + 1) * H * 4].bitcast(FP8X4)
                    rhs_scale = late["w1hs"][:, s * H : (s + 1) * H]
                else:
                    rhs = w1[e][:, s * H * 2 : (s + 1) * H * 2].bitcast(FP4X4)
                    a = (e - 1) * PASSES + s
                    rhs_scale = w1cs[:, a * H : (a + 1) * H]
                nc.tensor.matmul_mx(out=accs[half], lhsT=gw[e][:, cols].bitcast(FP8X4), lhsT_scale=token_scales(e, s, half),
                                    rhs=rhs, rhs_scale=rhs_scale, start=(s == 0), stop=(s == PASSES - 1))
            for half in range(C // P):
                relu = ring.tile([P, PACK, P], F32, name="relu")
                src = accs[half].rearrange("j (m t) -> j t m", t=PACK)
                if (e, half) in V_RELU:
                    nc.vector.tensor_scalar_max(out=relu[:], in0=src, scalar1=0.0)
                else:
                    nc.scalar.activation(out=relu[:], in_=src, func=ACT.Relu)
                turned = psum1.tile([P, PACK, P], F32, name="turned", bufs=2)
                for t in range(PACK):
                    nc.tensor.transpose(turned[:, t, :], relu[:, t, :], ident[:])
                late[e, half] = turned

        def square(e):
            for half in range(C // P):
                turned = late[e, half]
                nc.scalar.activation(
                    out=hb[e][:, half * P * PACK : (half + 1) * P * PACK].rearrange("m (j t) -> m j t", t=PACK),
                    in_=turned[:].rearrange("m t j -> m j t"), func=ACT.Square)

        def quantise_h(e):
            for j0, n in pieces(e):
                codes = ring.tile([P, n], U32, name="h_codes", align_bytes=64)
                scales = ring.tile([P, n], U8, name="h_scales", align_bytes=64)
                nc.vector.quantize_mx(out=codes[:].bitcast(FP8X4), scales=scales[:], in_=hb[e][:, j0 * PACK : (j0 + n) * PACK])
                hq[e, j0] = (codes, scales)

        def deal_w2(e, words, scales):
            w2s[e] = keep.tile([P, N], U8, name="w2s%d" % e, align_bytes=64)
            nc.vector.tensor_copy(out=w2s[e][:].rearrange("p (t m) -> p t m", t=PACK),
                                  in_=scales.rearrange("p (m t) -> p t m", t=PACK))
            w2[e] = keep.tile([P, N * (4 if e == 0 else 2)], U8, name="w2_%d" % e, align_bytes=64)
            word = U32 if e == 0 else U16
            (nc.vector.tensor_copy if e in (0,1,2,3,4) else nc.scalar.copy)(out=w2[e][:].bitcast(word).rearrange("p (t m) -> p t m", t=PACK),
                           in_=words.bitcast(word).rearrange("p (m t) -> p t m", t=PACK))

        def second_layer(e, j0, n):
            codes, scales = hq[e, j0]
            ysb[e, j0] = ring.tile([P, PACK, n], F32, name="ysb")
            per_bank = N // n
            for t0 in range(0, PACK, per_bank):
                acc = psum2.tile([P, per_bank, n], F32, name="acc2")
                for u in range(per_bank):
                    t = t0 + u
                    if e == 0:
                        lhsT = w2[e][:, 4 * t * P : 4 * (t + 1) * P].bitcast(FP8X4)
                    else:
                        lhsT = w2[e][:, 2 * t * P : 2 * (t + 1) * P].bitcast(FP4X4)
                    nc.tensor.matmul_mx(out=acc[:, u, :], lhsT=lhsT, lhsT_scale=w2s[e][:, t * P : (t + 1) * P],
                                        rhs=codes[:].bitcast(FP8X4), rhs_scale=scales[:], start=True, stop=True)
                if (e, j0, t0) in V_YEV:
                    nc.vector.tensor_copy(out=ysb[e, j0][:, t0 : t0 + per_bank, :], in_=acc[:])
                else:
                    nc.scalar.copy(out=ysb[e, j0][:, t0 : t0 + per_bank, :], in_=acc[:])
            nc.sync.dma_start(out=out_rows[:, :, e * C + j0 : e * C + j0 + n], in_=ysb[e, j0][:])

        def planes(e, j0, n):
            cols = slice(e * C + j0, e * C + j0 + n)
            yb = ring.tile([P, n * PACK], BF16, name="yb", align_bytes=64)
            nc.vector.tensor_copy(out=yb[:].rearrange("p (c i t) -> p c t i", i=4, t=PACK),
                                  in_=ysb[e, j0][:].rearrange("p t (c i) -> p c t i", i=4))
            y_codes = ring.tile([P, n], U32, name="y_codes", align_bytes=64)
            nc.vector.quantize_mx(out=y_codes[:].bitcast(FP8X4), scales=y_scales[:, cols], in_=yb[:])
            nc.sync.dma_start(out=out_words[:, cols], in_=y_codes[:].bitcast(I32))

        def finish(e):
            for j0, n in pieces(e):
                second_layer(e, j0, n)
                planes(e, j0, n)

        gather(ORDER[0])
        second = shared.tile([P, 12288], U8, name="second", align_bytes=64, offset=AT_LATE)
        w2cs_raw, w2c_raw = second[:, :2048], second[:, 2048:6144]
        nc.vector.memset(w2cs_raw.bitcast(I32), 0)
        load_scale_rows([nc.sync], w2cs_raw, w2c_scales.rearrange("f s b i -> (f s) b i"))
        nc.sync.dma_start(out=w2c_raw.bitcast(I32).rearrange("p (f w) -> p f w", f=COLD),
                          in_=w2c_words.rearrange("f s p c -> p (f s) c").bitcast(I32))
        for f in range(2, COLD):
            w1[1 + f] = second[:, f * 3072 : (f + 1) * 3072]
            nc.sync.dma_start(out=w1[1 + f].bitcast(I32).rearrange("p (s w) -> p s w", s=PASSES),
                              in_=w1c_words[f].rearrange("s p c -> p s c").bitcast(I32))
        gather(ORDER[1])
        gather(ORDER[2])
        for pos, e in enumerate(ORDER):
            first_layer(e)
            if pos >= 1:
                finish(ORDER[pos - 1])
            square(e)
            if pos == 1:
                w1[0] = shared.tile([P, PASSES * H * 4], U8, name="w1h", align_bytes=64, offset=AT_W1 - 6144 + 64)
                nc.sync.dma_start(out=w1[0][:].bitcast(I32).rearrange("p (s w) -> p s w", s=PASSES),
                                  in_=w1h_words[0].rearrange("s p i d -> p s (i d)").bitcast(I32))
                late["w1hs"] = shared.tile([P, PASSES * H], U8, name="w1hs", align_bytes=64, offset=AT_W1 + 6144 - 576 - 1536)
                nc.vector.memset(late["w1hs"][:].bitcast(I32), 0)
                load_scale_rows([nc.sync], late["w1hs"], w1h_scales[0])
                w2hs_raw = shared.tile([P, N], U8, name="w2hs_raw", align_bytes=64, offset=AT_W1 + 6144 - 576)
                nc.vector.memset(w2hs_raw[:].bitcast(I32), 0)
                load_scale_rows([nc.sync], w2hs_raw, w2h_scales[0])
                w2h_raw = shared.tile([P, N * 4], U8, name="w2h_raw", align_bytes=64, offset=AT_W1 + 6144 - 64)
                nc.sync.dma_start(out=w2h_raw[:].bitcast(I32), in_=w2h_words[0, 0].rearrange("p n d -> p (n d)").bitcast(I32))
            if e == 0:
                deal_w2(e, w2h_raw[:], w2hs_raw[:])
            else:
                deal_w2(e, w2c_raw[:, (e - 1) * N * 2 : e * N * 2], w2cs_raw[:, (e - 1) * N : e * N])
            quantise_h(e)
            if pos + 3 < E:
                gather(ORDER[pos + 3])
        for e in ORDER[E - 1 :]:
            finish(e)
        for q in range(4):
            queue = nc.scalar if q % 2 == 0 else nc.sync
            queue.dma_start(out=out_2[0, 4 * q : 4 * q + 4, :].bitcast(I32), in_=y_scales[32 * q : 32 * q + 4, :].bitcast(I32))
